import numpy as np
import ml_dtypes


def mxq(x, axis, fmt="e4m3"):
    dtype, down = {"e4m3": (ml_dtypes.float8_e4m3fn, 7), "e5m2": (ml_dtypes.float8_e5m2, 14)}[fmt]
    v = np.moveaxis(np.asarray(x, np.float32).astype(ml_dtypes.bfloat16).astype(np.float64), axis, -1)
    blocks = v.reshape(v.shape[:-1] + (-1, 32))
    amax = np.abs(blocks).max(-1, keepdims=True)
    byte = np.maximum(np.where(amax > 0, np.frexp(amax)[1] - 1 + 127, 0) - down, 1)
    scale = np.exp2(byte - 127.0)
    codes = (blocks / scale).astype(np.float32).astype(dtype).astype(np.float64)
    return np.moveaxis((codes * scale).reshape(v.shape), -1, axis)


WIDE = False


def mx_kscale(k):
    if not WIDE:
        return np.ones(k)
    levels = np.array([10, -10, 5, -5, 0])
    if k % 512:
        return np.exp2(np.random.permutation(np.resize(levels, k // 32))).repeat(32)
    a = np.empty((k // 512, 16))
    for p in range(k // 512):
        a[p, :8] = np.random.permutation(np.resize(levels, 8))
        for g in range(8):
            far = levels[np.abs(levels - a[p, g]) >= 10]
            a[p, g + 8] = far[np.random.randint(len(far))]
    return np.exp2(a.ravel()).repeat(32)


def f64(x):
    return np.asarray(x).astype(np.float64)


def striped(idx):
    return np.tile(idx.reshape(-1, 16).T, (8, 1)).astype(np.uint16)


def unstriped(offs):
    return offs[:16].T.reshape(-1).astype(np.int64)


def pack_weight(w):
    k, n = w.shape
    w = f64(np.asarray(w, np.float32).astype(ml_dtypes.bfloat16)).reshape(k // 32, 32, n)
    amax = np.abs(w).max(1)
    byte = np.clip(np.where(amax > 0, np.frexp(amax)[1] - 1 + 127 - 7, 1), 1, 254)
    scaled = (w * np.exp2(127.0 - byte)[:, None, :]).reshape(k, n).astype(np.float32)
    words = np.ascontiguousarray(scaled.reshape(k // 512, 128, 4, n).transpose(0, 1, 3, 2)).astype(ml_dtypes.float8_e4m3fn).view(np.uint8)
    return words, np.ascontiguousarray(byte.astype(np.uint8).reshape(k // 512, 16, n))


def unpack_weight(words, scales):
    g, p, n, _ = words.shape
    vals = np.ascontiguousarray(words).view(ml_dtypes.float8_e4m3fn).astype(np.float64) * np.repeat(np.exp2(scales.astype(np.float64) - 127.0), 8, axis=1)[..., None]
    return vals.transpose(0, 1, 3, 2).reshape(g * 512, n)


K, T, S, N, V, U = 512, 2048, 512, 256, 256, 512


def setup_inputs():
    n = np.random.standard_normal
    s = mx_kscale(K)[:, None]
    packed_xT = pack_weight(n((K, T)) * s)
    return {
        "x_words": packed_xT[0],
        "x_scales": packed_xT[1],
        "w1": (n((K, N)) / np.sqrt(K) / s).astype(np.float32),
        "bits": (np.where(np.random.uniform(size=(N, V)) < 0.5, 1.0, -1.0)).astype(np.float32),
        "offs": striped(np.random.permutation(T)[:S]),
        "left": striped(np.random.permutation(S)[:V]),
        "right": striped(np.random.permutation(S)[:V]),
        "par": striped(np.random.permutation(np.concatenate([np.arange(V), np.random.randint(0, V, U - V)]))),
    }


def reference(x_words, x_scales, w1, bits, offs, left, right, par):
    xq = unpack_weight(x_words, x_scales)[:, unstriped(offs)]
    y = mxq(f64(w1), 0, "e4m3").T @ xq
    d1 = y[:, unstriped(right)]
    a = y[:, unstriped(left)]
    gg = d1 + f64(bits) * a
    f = 0.5 * (np.abs(a + d1) - np.abs(a - d1))
    return gg[:, unstriped(par)] + 0.1 * f[:, unstriped(par)]

@@ -1,0 +1,124 @@
+from contextlib import ExitStack
+
+import concourse.mybir as mybir
+
+K, T, S, N, V, U = 512, 2048, 512, 256, 256, 512
+FLOPS = 2 * K * N * S
+
+F32 = mybir.dt.float32
+BF16 = mybir.dt.bfloat16
+I32 = mybir.dt.int32
+U32 = mybir.dt.uint32
+U16 = mybir.dt.uint16
+U8 = mybir.dt.uint8
+FP8X4 = mybir.dt.float8_e4m3fn_x4
+ALU = mybir.AluOpType
+ACT = mybir.ActivationFunctionType
+
+P = 128
+PACK = 4
+BLOCKS = N // P
+HALF = S // 2
+UP, DOWN, TENTH_HALF = 1.05, 0.95, 0.05
+
+
+def tile_picked_ypolar_bit_p_kernel(tc, x_words, x_scales, w1, bits, offs, left, right, par, out):
+    nc = tc.nc
+    with ExitStack() as ctx:
+        keep = ctx.enter_context(tc.tile_pool(name="keep", bufs=1))
+        psum = ctx.enter_context(tc.psum_pool(name="psum", bufs=1))
+
+        offs_sb = keep.tile([P, S // 16], U16, name="offs_sb")
+        left_sb = keep.tile([P, V // 16], U16, name="left_sb")
+        right_sb = keep.tile([P, V // 16], U16, name="right_sb")
+        par_sb = keep.tile([P, U // 16], U16, name="par_sb")
+        word_table = keep.tile([P, T], I32, name="word_table", align_bytes=64)
+        scale_table = keep.tile([P, T], U8, name="scale_table", align_bytes=64)
+        w_raw = keep.tile([P, PACK, N], F32, name="w_raw")
+        bits_sb = keep.tile([P, BLOCKS, V], F32, name="bits_sb")
+
+        w_rows = w1.rearrange("(p j) n -> p j n", j=PACK)
+        nc.vector.memset(scale_table[:].bitcast(I32), 0)
+        nc.sync.dma_start(offs_sb[:], offs)
+        nc.sync.dma_start(w_raw[:], w_rows)
+        nc.sync.dma_start(right_sb[:], right)
+        for r in range(4):
+            nc.sync.dma_start(scale_table[r:P:32, :].bitcast(I32), x_scales[0, r:16:4, :].bitcast(I32))
+        nc.sync.dma_start(word_table[:], x_words[0].rearrange("p n t -> p (n t)").bitcast(I32))
+        nc.sync.dma_start(bits_sb[:], bits.rearrange("(b p) v -> p b v", p=P))
+        nc.sync.dma_start(left_sb[:], left)
+        nc.sync.dma_start(par_sb[:], par)
+
+        w_bf = [keep.tile([P, P, PACK], BF16, name=f"w_bf{b}", align_bytes=64) for b in range(BLOCKS)]
+        w_codes = [keep.tile([P, P], U32, name=f"w_codes{b}", align_bytes=64) for b in range(BLOCKS)]
+        w_scales = [keep.tile([P, P], U8, name=f"w_scales{b}", align_bytes=64) for b in range(BLOCKS)]
+
+        def cast_w(b):
+            nc.scalar.activation(w_bf[b][:], w_raw[:, :, b * P : (b + 1) * P].rearrange("p j m -> p m j"), ACT.Copy)
+
+        def quantize_w(b):
+            nc.vector.quantize_mx(
+                out=w_codes[b][:].bitcast(FP8X4),
+                scales=w_scales[b][:],
+                in_=w_bf[b][:].rearrange("p m j -> p (m j)"),
+            )
+
+        x_scale = keep.tile([P, S], U8, name="x_scale", align_bytes=64)
+        x_code = [keep.tile([P, HALF], U32, name=f"x_code{h}", align_bytes=64) for h in range(2)]
+
+        cast_w(0)
+        cast_w(1)
+        nc.vector.tensor_copy(x_scale[:], scale_table[:].indirect(offs_sb[:]))
+        quantize_w(0)
+        quantize_w(1)
+        for h in range(2):
+            nc.vector.tensor_copy(
+                x_code[h][:], word_table[:].bitcast(U32).indirect(offs_sb[:, h * 16 : (h + 1) * 16])
+            )
+
+        y = [keep.tile([P, S], F32, name=f"y{b}") for b in range(BLOCKS)]
+        for h in range(2):
+            for b in range(BLOCKS):
+                acc = psum.tile([P, HALF], F32, name=f"acc{b}{h}")
+                nc.tensor.matmul_mx(
+                    out=acc[:],
+                    lhsT=w_codes[b][:].bitcast(FP8X4),
+                    lhsT_scale=w_scales[b][:],
+                    rhs=x_code[h][:].bitcast(FP8X4),
+                    rhs_scale=x_scale[:, h * HALF : (h + 1) * HALF],
+                    start=True,
+                    stop=True,
+                )
+                cols = y[b][:, h * HALF : (h + 1) * HALF]
+                if (b, h) == (0, 1):
+                    nc.vector.tensor_copy(cols, acc[:])
+                else:
+                    nc.scalar.copy(cols, acc[:])
+
+        blocks = range(BLOCKS)
+        bd = [keep.tile([P, V], F32, name=f"bd{b}") for b in blocks]
+        s = [keep.tile([P, V], F32, name=f"s{b}") for b in blocks]
+        abs_o = [keep.tile([P, V], F32, name=f"abs_o{b}") for b in blocks]
+        leaky = [keep.tile([P, V], F32, name=f"leaky{b}") for b in blocks]
+        hor = [keep.tile([P, 3, V], F32, name=f"hor{b}") for b in blocks]
+        res = [keep.tile([P, U], F32, name=f"res{b}") for b in blocks]
+
+        for b in blocks:
+            nc.vector.tensor_tensor(bd[b][:], y[b][:].indirect(right_sb[:]), bits_sb[:, b, :], ALU.mult)
+        for b in blocks:
+            nc.vector.tensor_tensor(s[b][:], y[b][:].indirect(left_sb[:]), bd[b][:], ALU.add)
+        for b in blocks:
+            nc.vector.scalar_tensor_tensor(hor[b][:, 1, :], bd[b][:], -2.0, s[b][:], ALU.mult, ALU.add)
+            nc.scalar.activation(abs_o[b][:], hor[b][:, 1, :], ACT.Abs, scale=TENTH_HALF / UP)
+        for b in blocks:
+            nc.vector.scalar_tensor_tensor(leaky[b][:], s[b][:], DOWN / UP, s[b][:], ALU.mult, ALU.max)
+        for b in blocks:
+            nc.vector.tensor_tensor(hor[b][:, 2, :], leaky[b][:], abs_o[b][:], ALU.subtract)
+        for b in blocks:
+            nc.vector.scalar_tensor_tensor(hor[b][:, 0, :], hor[b][:, 2, :], UP, bits_sb[:, b, :], ALU.mult, ALU.mult)
+        for b in blocks:
+            window = hor[b][:].rearrange("p c v -> p (c v)")
+            cuts = (0, U) if b == 0 else (0, U // 2, U)
+            for lo, hi in zip(cuts, cuts[1:]):
+                nc.vector.tensor_copy(res[b][:, lo:hi], window.indirect(par_sb[:, lo // 16 : hi // 16]))
+                nc.sync.dma_start(out[b * P : (b + 1) * P, lo:hi], res[b][:, lo:hi])

@@ -34,19 +34,22 @@ def tile_picked_ypolar_bit_p_kernel(tc, x_words, x_scales, w1, bits, offs, left,
         par_sb = keep.tile([P, U // 16], U16, name="par_sb")
         word_table = keep.tile([P, T], I32, name="word_table", align_bytes=64)
         scale_table = keep.tile([P, T], U8, name="scale_table", align_bytes=64)
-        w_raw = keep.tile([P, PACK, N], F32, name="w_raw")
-        bits_sb = keep.tile([P, BLOCKS, V], F32, name="bits_sb")
+        w_raw = [keep.tile([P, PACK, P], F32, name=f"w_raw{b}") for b in range(BLOCKS)]
+        bits_sb = [keep.tile([P, V], F32, name=f"bits_sb{b}") for b in range(BLOCKS)]
 
         w_rows = w1.rearrange("(p j) n -> p j n", j=PACK)
         nc.vector.memset(scale_table[:].bitcast(I32), 0)
         nc.sync.dma_start(offs_sb[:], offs)
-        nc.sync.dma_start(w_raw[:], w_rows)
+        nc.sync.dma_start(w_raw[0][:], w_rows[:, :, 0:P])
         nc.sync.dma_start(right_sb[:], right)
         for r in range(4):
-            nc.sync.dma_start(scale_table[r:P:32, :].bitcast(I32), x_scales[0, r:16:4, :].bitcast(I32))
+            queue = nc.sync if r < 2 else nc.scalar
+            queue.dma_start(scale_table[r:P:32, :].bitcast(I32), x_scales[0, r:16:4, :].bitcast(I32))
         nc.sync.dma_start(word_table[:], x_words[0].rearrange("p n t -> p (n t)").bitcast(I32))
-        nc.sync.dma_start(bits_sb[:], bits.rearrange("(b p) v -> p b v", p=P))
+        nc.sync.dma_start(w_raw[1][:], w_rows[:, :, P : 2 * P])
+        nc.sync.dma_start(bits_sb[0][:], bits[0:P, :])
         nc.sync.dma_start(left_sb[:], left)
+        nc.sync.dma_start(bits_sb[1][:], bits[P : 2 * P, :])
         nc.sync.dma_start(par_sb[:], par)
 
         w_bf = [keep.tile([P, P, PACK], BF16, name=f"w_bf{b}", align_bytes=64) for b in range(BLOCKS)]
@@ -54,7 +57,11 @@ def tile_picked_ypolar_bit_p_kernel(tc, x_words, x_scales, w1, bits, offs, left,
         w_scales = [keep.tile([P, P], U8, name=f"w_scales{b}", align_bytes=64) for b in range(BLOCKS)]
 
         def cast_w(b):
-            nc.scalar.activation(w_bf[b][:], w_raw[:, :, b * P : (b + 1) * P].rearrange("p j m -> p m j"), ACT.Copy)
+            nc.scalar.activation(
+                w_bf[b][:].rearrange("p (c i) j -> p c j i", i=4),
+                w_raw[b][:].rearrange("p j (c i) -> p c j i", i=4),
+                ACT.Copy,
+            )
 
         def quantize_w(b):
             nc.vector.quantize_mx(
@@ -64,36 +71,32 @@ def tile_picked_ypolar_bit_p_kernel(tc, x_words, x_scales, w1, bits, offs, left,
             )
 
         x_scale = keep.tile([P, S], U8, name="x_scale", align_bytes=64)
-        x_code = [keep.tile([P, HALF], U32, name=f"x_code{h}", align_bytes=64) for h in range(2)]
+        x_code = keep.tile([P, S], U32, name="x_code", align_bytes=64)
 
         cast_w(0)
-        cast_w(1)
         nc.vector.tensor_copy(x_scale[:], scale_table[:].indirect(offs_sb[:]))
         quantize_w(0)
+        for lo, hi in ((0, HALF), (HALF, S)):
+            nc.vector.tensor_copy(x_code[:, lo:hi], word_table[:].bitcast(U32).indirect(offs_sb[:, lo // 16 : hi // 16]))
+        cast_w(1)
         quantize_w(1)
-        for h in range(2):
-            nc.vector.tensor_copy(
-                x_code[h][:], word_table[:].bitcast(U32).indirect(offs_sb[:, h * 16 : (h + 1) * 16])
-            )
 
         y = [keep.tile([P, S], F32, name=f"y{b}") for b in range(BLOCKS)]
-        for h in range(2):
-            for b in range(BLOCKS):
-                acc = psum.tile([P, HALF], F32, name=f"acc{b}{h}")
+        for b in range(BLOCKS):
+            cuts = (0, HALF, HALF + P, S) if b == 0 else (0, HALF, S)
+            for i, (lo, hi) in enumerate(zip(cuts, cuts[1:])):
+                cols = slice(lo, hi)
+                acc = psum.tile([P, hi - lo], F32, name=f"acc{b}{i}")
                 nc.tensor.matmul_mx(
                     out=acc[:],
                     lhsT=w_codes[b][:].bitcast(FP8X4),
                     lhsT_scale=w_scales[b][:],
-                    rhs=x_code[h][:].bitcast(FP8X4),
-                    rhs_scale=x_scale[:, h * HALF : (h + 1) * HALF],
+                    rhs=x_code[:, cols].bitcast(FP8X4),
+                    rhs_scale=x_scale[:, cols],
                     start=True,
                     stop=True,
                 )
-                cols = y[b][:, h * HALF : (h + 1) * HALF]
-                if (b, h) == (0, 1):
-                    nc.vector.tensor_copy(cols, acc[:])
-                else:
-                    nc.scalar.copy(cols, acc[:])
+                nc.scalar.copy(y[b][:, cols], acc[:])
 
         blocks = range(BLOCKS)
         bd = [keep.tile([P, V], F32, name=f"bd{b}") for b in blocks]
@@ -104,7 +107,7 @@ def tile_picked_ypolar_bit_p_kernel(tc, x_words, x_scales, w1, bits, offs, left,
         res = [keep.tile([P, U], F32, name=f"res{b}") for b in blocks]
 
         for b in blocks:
-            nc.vector.tensor_tensor(bd[b][:], y[b][:].indirect(right_sb[:]), bits_sb[:, b, :], ALU.mult)
+            nc.vector.tensor_tensor(bd[b][:], y[b][:].indirect(right_sb[:]), bits_sb[b][:], ALU.mult)
         for b in blocks:
             nc.vector.tensor_tensor(s[b][:], y[b][:].indirect(left_sb[:]), bd[b][:], ALU.add)
         for b in blocks:
@@ -115,10 +118,10 @@ def tile_picked_ypolar_bit_p_kernel(tc, x_words, x_scales, w1, bits, offs, left,
         for b in blocks:
             nc.vector.tensor_tensor(hor[b][:, 2, :], leaky[b][:], abs_o[b][:], ALU.subtract)
         for b in blocks:
-            nc.vector.scalar_tensor_tensor(hor[b][:, 0, :], hor[b][:, 2, :], UP, bits_sb[:, b, :], ALU.mult, ALU.mult)
+            nc.vector.scalar_tensor_tensor(hor[b][:, 0, :], hor[b][:, 2, :], UP, bits_sb[b][:], ALU.mult, ALU.mult)
         for b in blocks:
             window = hor[b][:].rearrange("p c v -> p (c v)")
-            cuts = (0, U) if b == 0 else (0, U // 2, U)
+            cuts = (0, U) if b == 0 else (0, U - P, U)
             for lo, hi in zip(cuts, cuts[1:]):
                 nc.vector.tensor_copy(res[b][:, lo:hi], window.indirect(par_sb[:, lo // 16 : hi // 16]))
                 nc.sync.dma_start(out[b * P : (b + 1) * P, lo:hi], res[b][:, lo:hi])

@@ -81,6 +81,9 @@ def tile_picked_ypolar_bit_p_kernel(tc, x_words, x_scales, w1, bits, offs, left,
         cast_w(1)
         quantize_w(1)
 
+        gain = keep.tile([P, 1], F32, name="gain", tag="gain_then_s0")
+        nc.vector.memset(gain[:], 1.0)
+        nc.vector.tensor_scalar_mul(gain[:], gain[:], UP)
         y = [keep.tile([P, S], F32, name=f"y{b}") for b in range(BLOCKS)]
         for b in range(BLOCKS):
             cuts = (0, HALF, HALF + P, S) if b == 0 else (0, HALF, S)
@@ -96,11 +99,11 @@ def tile_picked_ypolar_bit_p_kernel(tc, x_words, x_scales, w1, bits, offs, left,
                     start=True,
                     stop=True,
                 )
-                nc.scalar.copy(y[b][:, cols], acc[:])
+                nc.scalar.activation(y[b][:, cols], acc[:], ACT.Copy, scale=gain[:])
 
         blocks = range(BLOCKS)
         bd = [keep.tile([P, V], F32, name=f"bd{b}") for b in blocks]
-        s = [keep.tile([P, V], F32, name=f"s{b}") for b in blocks]
+        s = [keep.tile([P, V], F32, name="s0", tag="gain_then_s0"), keep.tile([P, V], F32, name="s1")]
         abs_o = [keep.tile([P, V], F32, name=f"abs_o{b}") for b in blocks]
         leaky = [keep.tile([P, V], F32, name=f"leaky{b}") for b in blocks]
         hor = [keep.tile([P, 3, V], F32, name=f"hor{b}") for b in blocks]
@@ -118,7 +121,7 @@ def tile_picked_ypolar_bit_p_kernel(tc, x_words, x_scales, w1, bits, offs, left,
         for b in blocks:
             nc.vector.tensor_tensor(hor[b][:, 2, :], leaky[b][:], abs_o[b][:], ALU.subtract)
         for b in blocks:
-            nc.vector.scalar_tensor_tensor(hor[b][:, 0, :], hor[b][:, 2, :], UP, bits_sb[b][:], ALU.mult, ALU.mult)
+            nc.vector.tensor_tensor(hor[b][:, 0, :], hor[b][:, 2, :], bits_sb[b][:], ALU.mult)
         for b in blocks:
             window = hor[b][:].rearrange("p c v -> p (c v)")
             cuts = (0, U) if b == 0 else (0, U - P, U)

from contextlib import ExitStack

import concourse.mybir as mybir

K, T, S, N, V, U = 512, 2048, 512, 256, 256, 512
FLOPS = 2 * K * N * S

F32 = mybir.dt.float32
BF16 = mybir.dt.bfloat16
I32 = mybir.dt.int32
U32 = mybir.dt.uint32
U16 = mybir.dt.uint16
U8 = mybir.dt.uint8
FP8X4 = mybir.dt.float8_e4m3fn_x4
ALU = mybir.AluOpType
ACT = mybir.ActivationFunctionType

P = 128
PACK = 4
BLOCKS = N // P
HALF = S // 2
UP, DOWN, TENTH_HALF = 1.05, 0.95, 0.05


def tile_picked_ypolar_bit_p_kernel(tc, x_words, x_scales, w1, bits, offs, left, right, par, out):
    nc = tc.nc
    with ExitStack() as ctx:
        keep = ctx.enter_context(tc.tile_pool(name="keep", bufs=1))
        psum = ctx.enter_context(tc.psum_pool(name="psum", bufs=1))

        offs_sb = keep.tile([P, S // 16], U16, name="offs_sb")
        left_sb = keep.tile([P, V // 16], U16, name="left_sb")
        right_sb = keep.tile([P, V // 16], U16, name="right_sb")
        par_sb = keep.tile([P, U // 16], U16, name="par_sb")
        word_table = keep.tile([P, T], I32, name="word_table", align_bytes=64)
        scale_table = keep.tile([P, T], U8, name="scale_table", align_bytes=64)
        w_raw = [keep.tile([P, PACK, P], F32, name=f"w_raw{b}") for b in range(BLOCKS)]
        bits_sb = [keep.tile([P, V], F32, name=f"bits_sb{b}") for b in range(BLOCKS)]

        w_rows = w1.rearrange("(p j) n -> p j n", j=PACK)
        nc.vector.memset(scale_table[:].bitcast(I32), 0)
        nc.sync.dma_start(offs_sb[:], offs)
        nc.sync.dma_start(w_raw[0][:], w_rows[:, :, 0:P])
        nc.sync.dma_start(right_sb[:], right)
        for r in range(4):
            queue = nc.sync if r < 2 else nc.scalar
            queue.dma_start(scale_table[r:P:32, :].bitcast(I32), x_scales[0, r:16:4, :].bitcast(I32))
        nc.sync.dma_start(word_table[:], x_words[0].rearrange("p n t -> p (n t)").bitcast(I32))
        nc.sync.dma_start(w_raw[1][:], w_rows[:, :, P : 2 * P])
        nc.sync.dma_start(bits_sb[0][:], bits[0:P, :])
        nc.sync.dma_start(left_sb[:], left)
        nc.sync.dma_start(bits_sb[1][:], bits[P : 2 * P, :])
        nc.sync.dma_start(par_sb[:], par)

        w_bf = [keep.tile([P, P, PACK], BF16, name=f"w_bf{b}", align_bytes=64) for b in range(BLOCKS)]
        w_codes = [keep.tile([P, P], U32, name=f"w_codes{b}", align_bytes=64) for b in range(BLOCKS)]
        w_scales = [keep.tile([P, P], U8, name=f"w_scales{b}", align_bytes=64) for b in range(BLOCKS)]

        def cast_w(b):
            nc.scalar.activation(
                w_bf[b][:].rearrange("p (c i) j -> p c j i", i=4),
                w_raw[b][:].rearrange("p j (c i) -> p c j i", i=4),
                ACT.Copy,
            )

        def quantize_w(b):
            nc.vector.quantize_mx(
                out=w_codes[b][:].bitcast(FP8X4),
                scales=w_scales[b][:],
                in_=w_bf[b][:].rearrange("p m j -> p (m j)"),
            )

        x_scale = keep.tile([P, S], U8, name="x_scale", align_bytes=64)
        x_code = keep.tile([P, S], U32, name="x_code", align_bytes=64)

        cast_w(0)
        nc.vector.tensor_copy(x_scale[:], scale_table[:].indirect(offs_sb[:]))
        quantize_w(0)
        for lo, hi in ((0, HALF), (HALF, S)):
            nc.vector.tensor_copy(x_code[:, lo:hi], word_table[:].bitcast(U32).indirect(offs_sb[:, lo // 16 : hi // 16]))
        cast_w(1)
        quantize_w(1)

        gain = keep.tile([P, 1], F32, name="gain", tag="gain_then_s0")
        nc.vector.memset(gain[:], 1.0)
        nc.vector.tensor_scalar_mul(gain[:], gain[:], UP)
        y = [keep.tile([P, S], F32, name=f"y{b}") for b in range(BLOCKS)]
        for b in range(BLOCKS):
            cuts = (0, HALF, HALF + P, S) if b == 0 else (0, HALF, S)
            for i, (lo, hi) in enumerate(zip(cuts, cuts[1:])):
                cols = slice(lo, hi)
                acc = psum.tile([P, hi - lo], F32, name=f"acc{b}{i}")
                nc.tensor.matmul_mx(
                    out=acc[:],
                    lhsT=w_codes[b][:].bitcast(FP8X4),
                    lhsT_scale=w_scales[b][:],
                    rhs=x_code[:, cols].bitcast(FP8X4),
                    rhs_scale=x_scale[:, cols],
                    start=True,
                    stop=True,
                )
                nc.scalar.activation(y[b][:, cols], acc[:], ACT.Copy, scale=gain[:])

        blocks = range(BLOCKS)
        bd = [keep.tile([P, V], F32, name=f"bd{b}") for b in blocks]
        s = [keep.tile([P, V], F32, name="s0", tag="gain_then_s0"), keep.tile([P, V], F32, name="s1")]
        abs_o = [keep.tile([P, V], F32, name=f"abs_o{b}") for b in blocks]
        leaky = [keep.tile([P, V], F32, name=f"leaky{b}") for b in blocks]
        hor = [keep.tile([P, 3, V], F32, name=f"hor{b}") for b in blocks]
        res = [keep.tile([P, U], F32, name=f"res{b}") for b in blocks]

        for b in blocks:
            nc.vector.tensor_tensor(bd[b][:], y[b][:].indirect(right_sb[:]), bits_sb[b][:], ALU.mult)
        for b in blocks:
            nc.vector.tensor_tensor(s[b][:], y[b][:].indirect(left_sb[:]), bd[b][:], ALU.add)
        for b in blocks:
            nc.vector.scalar_tensor_tensor(hor[b][:, 1, :], bd[b][:], -2.0, s[b][:], ALU.mult, ALU.add)
            nc.scalar.activation(abs_o[b][:], hor[b][:, 1, :], ACT.Abs, scale=TENTH_HALF / UP)
        for b in blocks:
            nc.vector.scalar_tensor_tensor(leaky[b][:], s[b][:], DOWN / UP, s[b][:], ALU.mult, ALU.max)
        for b in blocks:
            nc.vector.tensor_tensor(hor[b][:, 2, :], leaky[b][:], abs_o[b][:], ALU.subtract)
        for b in blocks:
            nc.vector.tensor_tensor(hor[b][:, 0, :], hor[b][:, 2, :], bits_sb[b][:], ALU.mult)
        for b in blocks:
            window = hor[b][:].rearrange("p c v -> p (c v)")
            cuts = (0, U) if b == 0 else (0, U - P, U)
            for lo, hi in zip(cuts, cuts[1:]):
                nc.vector.tensor_copy(res[b][:, lo:hi], window.indirect(par_sb[:, lo // 16 : hi // 16]))
                nc.sync.dma_start(out[b * P : (b + 1) * P, lo:hi], res[b][:, lo:hi])
